import numpy as np
import ml_dtypes


def mxq(x, axis, fmt="e4m3"):
    dtype, down = {"e4m3": (ml_dtypes.float8_e4m3fn, 7), "e5m2": (ml_dtypes.float8_e5m2, 14)}[fmt]
    v = np.moveaxis(np.asarray(x, np.float32).astype(ml_dtypes.bfloat16).astype(np.float64), axis, -1)
    blocks = v.reshape(v.shape[:-1] + (-1, 32))
    amax = np.abs(blocks).max(-1, keepdims=True)
    byte = np.maximum(np.where(amax > 0, np.frexp(amax)[1] - 1 + 127, 0) - down, 1)
    scale = np.exp2(byte - 127.0)
    codes = (blocks / scale).astype(np.float32).astype(dtype).astype(np.float64)
    return np.moveaxis((codes * scale).reshape(v.shape), -1, axis)


WIDE = False


def mx_kscale(k):
    if not WIDE:
        return np.ones(k)
    levels = np.array([10, -10, 5, -5, 0])
    if k % 512:
        return np.exp2(np.random.permutation(np.resize(levels, k // 32))).repeat(32)
    a = np.empty((k // 512, 16))
    for p in range(k // 512):
        a[p, :8] = np.random.permutation(np.resize(levels, 8))
        for g in range(8):
            far = levels[np.abs(levels - a[p, g]) >= 10]
            a[p, g + 8] = far[np.random.randint(len(far))]
    return np.exp2(a.ravel()).repeat(32)


def f64(x):
    return np.asarray(x).astype(np.float64)


def striped(idx):
    return np.tile(np.asarray(idx).reshape(-1, 16).T, (8, 1)).astype(np.uint16)


def unstriped(offs):
    return offs[:16].T.reshape(-1).astype(np.int64)


E2M1 = np.array([0.0, 0.5, 1.0, 1.5, 2.0, 3.0, 4.0, 6.0, -0.0, -0.5, -1.0, -1.5, -2.0, -3.0, -4.0, -6.0])


def pack_weight(w, fmt):
    k, n = w.shape
    w = f64(np.asarray(w, np.float32).astype(ml_dtypes.bfloat16)).reshape(k // 32, 32, n)
    amax = np.abs(w).max(1)
    if fmt == "e4m3":
        byte = np.frexp(amax)[1] - 1 + 127 - 7
    else:
        mant, ex = np.frexp(amax / 6.0)
        byte = np.where(mant > 0.5, ex, ex - 1) + 127
    byte = np.clip(np.where(amax > 0, byte, 1), 1, 254)
    scaled = (w * np.exp2(127.0 - byte)[:, None, :]).reshape(k, n).astype(np.float32)
    by_word = np.ascontiguousarray(scaled.reshape(k // 512, 128, 4, n).transpose(0, 1, 3, 2))
    if fmt == "e4m3":
        words = by_word.astype(ml_dtypes.float8_e4m3fn).view(np.uint8)
    else:
        c = by_word.astype(ml_dtypes.float4_e2m1fn).view(np.uint8) & 0xF
        words = (c[..., 0::2] | (c[..., 1::2] << 4)).reshape(k // 512, 128, 2 * n)
    return np.ascontiguousarray(words), np.ascontiguousarray(byte.astype(np.uint8).reshape(k // 512, 16, n))


def unpack_weight(words, scales, fmt):
    g, _, n = scales.shape
    words = np.ascontiguousarray(words).reshape(g, 128, n, -1)
    if fmt == "e4m3":
        vals = words.view(ml_dtypes.float8_e4m3fn).astype(np.float64)
    else:
        nib = np.empty((g, 128, n, 4), np.uint8)
        nib[..., 0::2] = words & 0xF
        nib[..., 1::2] = words >> 4
        vals = E2M1[nib]
    vals = vals * np.repeat(np.exp2(scales.astype(np.float64) - 127.0), 8, axis=1)[..., None]
    return vals.transpose(0, 1, 3, 2).reshape(g * 512, n)


B, N, T, D, NQ = 1, 512, 2048, 512, 256


def setup_inputs():
    n = np.random.standard_normal
    idx = np.random.permutation(T)[:B * N]
    s = mx_kscale(D)[:, None]
    kp = pack_weight(n((D, T)) / s, "e4m3")
    cp = pack_weight(n((D, T)) / s, "e4m3")
    return {
        "qT": (n((B, D, NQ)) * s * (1.00 / np.sqrt(D))).astype(np.float32),
        "k_words": kp[0],
        "k_scales": kp[1],
        "c_words": cp[0],
        "c_scales": cp[1],
        "offs": striped(idx),
    }


def reference(qT, k_words, k_scales, c_words, c_scales, offs):
    idx = unstriped(offs)
    pick = lambda x, which: x[:, which].reshape(x.shape[0], B, -1).transpose(1, 0, 2)
    k = unpack_weight(k_words, k_scales, "e4m3")
    kg = pick(k, idx)
    c = unpack_weight(c_words, c_scales, "e4m3")
    cg = pick(c, idx)
    qq = mxq(f64(qT), 1, "e4m3")
    a = qq.transpose(0, 2, 1) @ kg
    z = qq.transpose(0, 2, 1) @ cg
    g = 1.5 * a - 0.5 * z
    m = np.max(g, axis=-1, keepdims=True)
    e = np.exp(g - m)
    y = e / np.sum(e, axis=-1, keepdims=True)
    return y

@@ -1,0 +1,114 @@
+from contextlib import ExitStack
+
+import concourse.mybir as mybir
+
+N, T, D, NQ = 512, 2048, 512, 256
+FLOPS = 2 * 2 * NQ * N * D
+
+F32 = mybir.dt.float32
+BF16 = mybir.dt.bfloat16
+I32 = mybir.dt.int32
+U32 = mybir.dt.uint32
+U16 = mybir.dt.uint16
+U8 = mybir.dt.uint8
+FP8X4 = mybir.dt.float8_e4m3fn_x4
+ALU = mybir.AluOpType
+ACT = mybir.ActivationFunctionType
+AX = mybir.AxisListType
+
+P = 128
+PACK = 4
+HALF = N // 2
+C_ROW = 4
+
+
+def tile_attend_cfg_topk_kernel(tc, qT, k_words, k_scales, c_words, c_scales, offs, out):
+    nc = tc.nc
+    with ExitStack() as ctx:
+        pool = ctx.enter_context(tc.tile_pool(name="sbuf", bufs=1))
+        psum = ctx.enter_context(tc.psum_pool(name="psum", bufs=1))
+
+        offsets = pool.tile([P, N // 16], U16, name="offsets")
+        nc.sync.dma_start(offsets[:], offs)
+
+        ks_all = pool.tile([P, T // 4], I32, name="ks_all")
+        cs_all = pool.tile([P, T // 4], I32, name="cs_all")
+        nc.vector.memset(ks_all[:], 0)
+        nc.gpsimd.memset(cs_all[:], 0)
+        ks_rows = k_scales[0].bitcast(I32)
+        cs_rows = c_scales[0].bitcast(I32)
+        for r in range(4):
+            nc.sync.dma_start(out=ks_all[r:P:32, :], in_=ks_rows[r:16:4, :])
+        for r in range(4):
+            queue = nc.sync if r < 2 else nc.gpsimd
+            queue.dma_start(out=cs_all[C_ROW + r:P:32, :], in_=cs_rows[r:16:4, :])
+
+        q_raw = pool.tile([P, PACK, NQ], F32, name="q_raw")
+        nc.scalar.dma_start(out=q_raw[:], in_=qT[0].rearrange("(p j) w -> p j w", j=PACK))
+        kw_all = pool.tile([P, T], I32, name="kw_all")
+        nc.scalar.dma_start(out=kw_all[:], in_=k_words[0].rearrange("p t r -> p (t r)").bitcast(I32))
+        cw_all = pool.tile([P, T], I32, name="cw_all")
+        nc.scalar.dma_start(out=cw_all[:], in_=c_words[0].rearrange("p t r -> p (t r)").bitcast(I32))
+
+        warm_in = pool.tile([P, 1], F32, name="warm_in")
+        warm_out = pool.tile([P, 1], F32, name="warm_out")
+        nc.vector.memset(warm_in[:], 0.0)
+        nc.scalar.activation(out=warm_out[:], in_=warm_in[:], func=ACT.Exp)
+
+        q_grouped = pool.tile([P, NQ, PACK], BF16, name="q_grouped", align_bytes=64)
+        nc.scalar.copy(out=q_grouped[:], in_=q_raw[:].rearrange("p j w -> p w j"))
+
+        ks = pool.tile([P, N], U8, name="ks", align_bytes=64)
+        nc.vector.tensor_copy(ks[:], ks_all[:].bitcast(U8).indirect(offsets[:]))
+
+        q_codes = pool.tile([P, NQ], U32, name="q_codes", align_bytes=64)
+        q_scales = pool.tile([P, NQ], U8, name="q_scales", align_bytes=64)
+        nc.vector.quantize_mx(out=q_codes[:].bitcast(FP8X4), scales=q_scales[:],
+                              in_=q_grouped[:].rearrange("p w j -> p (w j)"))
+
+        kw = pool.tile([P, N], U32, name="kw", align_bytes=64)
+        nc.vector.tensor_copy(kw[:], kw_all[:].bitcast(U32).indirect(offsets[:]))
+        cs = pool.tile([P, N], U8, name="cs", align_bytes=64)
+        nc.vector.tensor_copy(cs[:], cs_all[:].bitcast(U8).indirect(offsets[:]))
+
+        def scores(acc, b, words, scales):
+            cols = slice(b * P, (b + 1) * P)
+            nc.tensor.matmul_mx(out=acc, lhsT=q_codes[:, cols].bitcast(FP8X4), lhsT_scale=q_scales[:, cols],
+                                rhs=words.bitcast(FP8X4), rhs_scale=scales, start=True, stop=True)
+
+        a_neg = pool.tile([P, 2, N], F32, name="a_neg")
+        for b in range(2):
+            a = psum.tile([P, N], F32, name=f"a{b}")
+            scores(a[:], b, kw[:], ks[:])
+            nc.scalar.activation(out=a_neg[:, b, :], in_=a[:], func=ACT.Copy, scale=-1.5)
+
+        cw = [pool.tile([P, HALF], U32, name=f"cw{h}", align_bytes=64) for h in range(2)]
+        for h in range(2):
+            nc.vector.tensor_copy(cw[h][:], cw_all[:].bitcast(U32).indirect(offsets[:, h * 16:(h + 1) * 16]))
+
+        g_neg = pool.tile([P, 2, N], F32, name="g_neg")
+        z_first = psum.tile([P, 2, HALF], F32, name="z_first")
+        for b in range(2):
+            scores(z_first[:, b, :], b, cw[0][:], cs[C_ROW:P, 0:HALF])
+        z_second = [psum.tile([P, HALF], F32, name=f"z_second{b}") for b in range(2)]
+        for b in range(2):
+            scores(z_second[b][:], b, cw[1][:], cs[C_ROW:P, HALF:N])
+        nc.vector.scalar_tensor_tensor(out=g_neg[:, :, 0:HALF], in0=z_first[:], scalar=0.5,
+                                       in1=a_neg[:, :, 0:HALF], op0=ALU.mult, op1=ALU.add)
+        for b in range(2):
+            nc.vector.scalar_tensor_tensor(out=g_neg[:, b, HALF:N], in0=z_second[b][:], scalar=0.5,
+                                           in1=a_neg[:, b, HALF:N], op0=ALU.mult, op1=ALU.add)
+
+        m_neg = [pool.tile([P, 1], F32, name=f"m_neg{b}") for b in range(2)]
+        for b in range(2):
+            nc.vector.tensor_reduce(out=m_neg[b][:], in_=g_neg[:, b, :], axis=AX.X, op=ALU.min)
+        for b in range(2):
+            e = pool.tile([P, N], F32, name=f"e{b}")
+            total = pool.tile([P, 1], F32, name=f"total{b}")
+            inv = pool.tile([P, 1], F32, name=f"inv{b}")
+            y = pool.tile([P, N], F32, name=f"y{b}")
+            nc.scalar.activation(out=e[:], in_=g_neg[:, b, :], func=ACT.Exp, bias=m_neg[b][:], scale=-1.0,
+                                 accum_out=total[:])
+            nc.vector.reciprocal(out=inv[:], in_=total[:])
+            nc.vector.tensor_scalar(out=y[:], in0=e[:], scalar1=inv[:], scalar2=None, op0=ALU.mult)
+            nc.sync.dma_start(out=out[0, b * P:(b + 1) * P, :], in_=y[:])

@@ -31,32 +31,35 @@ def tile_attend_cfg_topk_kernel(tc, qT, k_words, k_scales, c_words, c_scales, of
         offsets = pool.tile([P, N // 16], U16, name="offsets")
         nc.sync.dma_start(offsets[:], offs)
 
+        kw_all = pool.tile([P, T], I32, name="kw_all")
+        nc.scalar.dma_start(out=kw_all[:], in_=k_words[0].rearrange("p t r -> p (t r)").bitcast(I32))
+        q_raw = pool.tile([P, PACK, NQ], F32, name="q_raw", tag="staging")
+        nc.scalar.dma_start(out=q_raw[:], in_=qT[0].rearrange("(p j) w -> p j w", j=PACK))
+        kw_all = pool.tile([P, T], I32, name="kw_all")
+        nc.scalar.dma_start(out=kw_all[:], in_=k_words[0].rearrange("p t r -> p (t r)").bitcast(I32))
+
+        warm_in = pool.tile([P, 1], F32, name="warm_in")
+        warm_out = pool.tile([P, 1], F32, name="warm_out")
+        nc.gpsimd.memset(warm_in[:], 0.0)
+        nc.scalar.activation(out=warm_out[:], in_=warm_in[:], func=ACT.Exp)
+
         ks_all = pool.tile([P, T // 4], I32, name="ks_all")
         cs_all = pool.tile([P, T // 4], I32, name="cs_all")
         nc.vector.memset(ks_all[:], 0)
-        nc.gpsimd.memset(cs_all[:], 0)
+        nc.vector.memset(cs_all[:], 0)
         ks_rows = k_scales[0].bitcast(I32)
         cs_rows = c_scales[0].bitcast(I32)
         for r in range(4):
             nc.sync.dma_start(out=ks_all[r:P:32, :], in_=ks_rows[r:16:4, :])
         for r in range(4):
-            queue = nc.sync if r < 2 else nc.gpsimd
-            queue.dma_start(out=cs_all[C_ROW + r:P:32, :], in_=cs_rows[r:16:4, :])
-
-        q_raw = pool.tile([P, PACK, NQ], F32, name="q_raw")
-        nc.scalar.dma_start(out=q_raw[:], in_=qT[0].rearrange("(p j) w -> p j w", j=PACK))
-        kw_all = pool.tile([P, T], I32, name="kw_all")
-        nc.scalar.dma_start(out=kw_all[:], in_=k_words[0].rearrange("p t r -> p (t r)").bitcast(I32))
-        cw_all = pool.tile([P, T], I32, name="cw_all")
-        nc.scalar.dma_start(out=cw_all[:], in_=c_words[0].rearrange("p t r -> p (t r)").bitcast(I32))
-
-        warm_in = pool.tile([P, 1], F32, name="warm_in")
-        warm_out = pool.tile([P, 1], F32, name="warm_out")
-        nc.vector.memset(warm_in[:], 0.0)
-        nc.scalar.activation(out=warm_out[:], in_=warm_in[:], func=ACT.Exp)
+            nc.sync.dma_start(out=cs_all[C_ROW + r:P:32, :], in_=cs_rows[r:16:4, :])
 
         q_grouped = pool.tile([P, NQ, PACK], BF16, name="q_grouped", align_bytes=64)
-        nc.scalar.copy(out=q_grouped[:], in_=q_raw[:].rearrange("p j w -> p w j"))
+        nc.vector.tensor_copy(out=q_grouped[:].rearrange("p (c i) j -> p c j i", i=4),
+                              in_=q_raw[:].rearrange("p j (c i) -> p c j i", i=4))
+
+        cw_all = pool.tile([P, T], I32, name="cw_all", tag="staging")
+        nc.scalar.dma_start(out=cw_all[:], in_=c_words[0].rearrange("p t r -> p (t r)").bitcast(I32))
 
         ks = pool.tile([P, N], U8, name="ks", align_bytes=64)
         nc.vector.tensor_copy(ks[:], ks_all[:].bitcast(U8).indirect(offsets[:]))

@@ -31,15 +31,11 @@ def tile_attend_cfg_topk_kernel(tc, qT, k_words, k_scales, c_words, c_scales, of
         offsets = pool.tile([P, N // 16], U16, name="offsets")
         nc.sync.dma_start(offsets[:], offs)
 
-        kw_all = pool.tile([P, T], I32, name="kw_all")
-        nc.scalar.dma_start(out=kw_all[:], in_=k_words[0].rearrange("p t r -> p (t r)").bitcast(I32))
-        q_raw = pool.tile([P, PACK, NQ], F32, name="q_raw", tag="staging")
+        q_raw = pool.tile([P, PACK, NQ], F32, name="q_raw", tag="q_then_c")
         nc.scalar.dma_start(out=q_raw[:], in_=qT[0].rearrange("(p j) w -> p j w", j=PACK))
-        kw_all = pool.tile([P, T], I32, name="kw_all")
-        nc.scalar.dma_start(out=kw_all[:], in_=k_words[0].rearrange("p t r -> p (t r)").bitcast(I32))
 
         warm_in = pool.tile([P, 1], F32, name="warm_in")
-        warm_out = pool.tile([P, 1], F32, name="warm_out")
+        warm_out = pool.tile([P, 1], F32, name="warm_out", tag="warm_then_k")
         nc.gpsimd.memset(warm_in[:], 0.0)
         nc.scalar.activation(out=warm_out[:], in_=warm_in[:], func=ACT.Exp)
 
@@ -51,14 +47,16 @@ def tile_attend_cfg_topk_kernel(tc, qT, k_words, k_scales, c_words, c_scales, of
         cs_rows = c_scales[0].bitcast(I32)
         for r in range(4):
             nc.sync.dma_start(out=ks_all[r:P:32, :], in_=ks_rows[r:16:4, :])
+        kw_all = pool.tile([P, T], I32, name="kw_all", tag="warm_then_k")
+        nc.scalar.dma_start(out=kw_all[:], in_=k_words[0].rearrange("p t r -> p (t r)").bitcast(I32))
         for r in range(4):
-            nc.sync.dma_start(out=cs_all[C_ROW + r:P:32, :], in_=cs_rows[r:16:4, :])
+            nc.scalar.dma_start(out=cs_all[C_ROW + r:P:32, :], in_=cs_rows[r:16:4, :])
 
         q_grouped = pool.tile([P, NQ, PACK], BF16, name="q_grouped", align_bytes=64)
         nc.vector.tensor_copy(out=q_grouped[:].rearrange("p (c i) j -> p c j i", i=4),
                               in_=q_raw[:].rearrange("p j (c i) -> p c j i", i=4))
 
-        cw_all = pool.tile([P, T], I32, name="cw_all", tag="staging")
+        cw_all = pool.tile([P, T], I32, name="cw_all", tag="q_then_c")
         nc.scalar.dma_start(out=cw_all[:], in_=c_words[0].rearrange("p t r -> p (t r)").bitcast(I32))
 
         ks = pool.tile([P, N], U8, name="ks", align_bytes=64)

@@ -31,33 +31,28 @@ def tile_attend_cfg_topk_kernel(tc, qT, k_words, k_scales, c_words, c_scales, of
         offsets = pool.tile([P, N // 16], U16, name="offsets")
         nc.sync.dma_start(offsets[:], offs)
 
-        q_raw = pool.tile([P, PACK, NQ], F32, name="q_raw", tag="q_then_c")
+        q_raw = pool.tile([P, PACK, NQ], F32, name="q_raw")
         nc.scalar.dma_start(out=q_raw[:], in_=qT[0].rearrange("(p j) w -> p j w", j=PACK))
-
-        warm_in = pool.tile([P, 1], F32, name="warm_in")
-        warm_out = pool.tile([P, 1], F32, name="warm_out", tag="warm_then_k")
-        nc.gpsimd.memset(warm_in[:], 0.0)
-        nc.scalar.activation(out=warm_out[:], in_=warm_in[:], func=ACT.Exp)
 
         ks_all = pool.tile([P, T // 4], I32, name="ks_all")
         cs_all = pool.tile([P, T // 4], I32, name="cs_all")
-        nc.vector.memset(ks_all[:], 0)
+        nc.vector.memset(ks_all[:, 0:T // 8], 0)
+        nc.gpsimd.memset(ks_all[:, T // 8:T // 4], 0)
         nc.vector.memset(cs_all[:], 0)
         ks_rows = k_scales[0].bitcast(I32)
         cs_rows = c_scales[0].bitcast(I32)
         for r in range(4):
             nc.sync.dma_start(out=ks_all[r:P:32, :], in_=ks_rows[r:16:4, :])
-        kw_all = pool.tile([P, T], I32, name="kw_all", tag="warm_then_k")
-        nc.scalar.dma_start(out=kw_all[:], in_=k_words[0].rearrange("p t r -> p (t r)").bitcast(I32))
+        kw_all = pool.tile([P, T], I32, name="kw_all")
+        nc.sync.dma_start(out=kw_all[:], in_=k_words[0].rearrange("p t r -> p (t r)").bitcast(I32))
         for r in range(4):
-            nc.scalar.dma_start(out=cs_all[C_ROW + r:P:32, :], in_=cs_rows[r:16:4, :])
+            nc.sync.dma_start(out=cs_all[C_ROW + r:P:32, :], in_=cs_rows[r:16:4, :])
+        cw_all = pool.tile([P, T], I32, name="cw_all")
+        nc.sync.dma_start(out=cw_all[:], in_=c_words[0].rearrange("p t r -> p (t r)").bitcast(I32))
 
         q_grouped = pool.tile([P, NQ, PACK], BF16, name="q_grouped", align_bytes=64)
-        nc.vector.tensor_copy(out=q_grouped[:].rearrange("p (c i) j -> p c j i", i=4),
-                              in_=q_raw[:].rearrange("p j (c i) -> p c j i", i=4))
-
-        cw_all = pool.tile([P, T], I32, name="cw_all", tag="q_then_c")
-        nc.scalar.dma_start(out=cw_all[:], in_=c_words[0].rearrange("p t r -> p (t r)").bitcast(I32))
+        nc.scalar.copy(out=q_grouped[:].rearrange("p (c i) j -> p c j i", i=4),
+                       in_=q_raw[:].rearrange("p j (c i) -> p c j i", i=4))
 
         ks = pool.tile([P, N], U8, name="ks", align_bytes=64)
         nc.vector.tensor_copy(ks[:], ks_all[:].bitcast(U8).indirect(offsets[:]))

@@ -32,7 +32,8 @@ def tile_attend_cfg_topk_kernel(tc, qT, k_words, k_scales, c_words, c_scales, of
         nc.sync.dma_start(offsets[:], offs)
 
         q_raw = pool.tile([P, PACK, NQ], F32, name="q_raw")
-        nc.scalar.dma_start(out=q_raw[:], in_=qT[0].rearrange("(p j) w -> p j w", j=PACK))
+        q_rows = qT[0].rearrange("(p j) w -> p j w", j=PACK)
+        nc.scalar.dma_start(out=q_raw[:, 0:2, :], in_=q_rows[:, 0:2, :])
 
         ks_all = pool.tile([P, T // 4], I32, name="ks_all")
         cs_all = pool.tile([P, T // 4], I32, name="cs_all")
@@ -42,7 +43,9 @@ def tile_attend_cfg_topk_kernel(tc, qT, k_words, k_scales, c_words, c_scales, of
         ks_rows = k_scales[0].bitcast(I32)
         cs_rows = c_scales[0].bitcast(I32)
         for r in range(4):
-            nc.sync.dma_start(out=ks_all[r:P:32, :], in_=ks_rows[r:16:4, :])
+            queue = nc.sync if r % 2 == 0 else nc.scalar
+            queue.dma_start(out=ks_all[r:P:32, :], in_=ks_rows[r:16:4, :])
+        nc.sync.dma_start(out=q_raw[:, 2:4, :], in_=q_rows[:, 2:4, :])
         kw_all = pool.tile([P, T], I32, name="kw_all")
         nc.sync.dma_start(out=kw_all[:], in_=k_words[0].rearrange("p t r -> p (t r)").bitcast(I32))
         for r in range(4):
@@ -51,8 +54,9 @@ def tile_attend_cfg_topk_kernel(tc, qT, k_words, k_scales, c_words, c_scales, of
         nc.sync.dma_start(out=cw_all[:], in_=c_words[0].rearrange("p t r -> p (t r)").bitcast(I32))
 
         q_grouped = pool.tile([P, NQ, PACK], BF16, name="q_grouped", align_bytes=64)
-        nc.scalar.copy(out=q_grouped[:].rearrange("p (c i) j -> p c j i", i=4),
-                       in_=q_raw[:].rearrange("p j (c i) -> p c j i", i=4))
+        for j in (0, 2):
+            nc.scalar.copy(out=q_grouped[:, :, j:j + 2].rearrange("p (c i) j -> p c j i", i=4),
+                           in_=q_raw[:, j:j + 2, :].rearrange("p j (c i) -> p c j i", i=4))
 
         ks = pool.tile([P, N], U8, name="ks", align_bytes=64)
         nc.vector.tensor_copy(ks[:], ks_all[:].bitcast(U8).indirect(offsets[:]))

@@ -28,48 +28,53 @@ def tile_attend_cfg_topk_kernel(tc, qT, k_words, k_scales, c_words, c_scales, of
         pool = ctx.enter_context(tc.tile_pool(name="sbuf", bufs=1))
         psum = ctx.enter_context(tc.psum_pool(name="psum", bufs=1))
 
+        q_raw = pool.tile([P, PACK, NQ], F32, name="q_raw")
+        q_rows = qT[0].rearrange("(p j) w -> p j w", j=PACK)
+        nc.sync.dma_start(out=q_raw[:, 0:2, :], in_=q_rows[:, 0:2, :])
         offsets = pool.tile([P, N // 16], U16, name="offsets")
         nc.sync.dma_start(offsets[:], offs)
 
-        q_raw = pool.tile([P, PACK, NQ], F32, name="q_raw")
-        q_rows = qT[0].rearrange("(p j) w -> p j w", j=PACK)
-        nc.scalar.dma_start(out=q_raw[:, 0:2, :], in_=q_rows[:, 0:2, :])
-
         ks_all = pool.tile([P, T // 4], I32, name="ks_all")
         cs_all = pool.tile([P, T // 4], I32, name="cs_all")
-        nc.vector.memset(ks_all[:, 0:T // 8], 0)
-        nc.gpsimd.memset(ks_all[:, T // 8:T // 4], 0)
+        nc.vector.memset(ks_all[:], 0)
         nc.vector.memset(cs_all[:], 0)
-        ks_rows = k_scales[0].bitcast(I32)
-        cs_rows = c_scales[0].bitcast(I32)
-        for r in range(4):
-            queue = nc.sync if r % 2 == 0 else nc.scalar
-            queue.dma_start(out=ks_all[r:P:32, :], in_=ks_rows[r:16:4, :])
+        nc.sync.dma_start(out=ks_all[0:P:8, :], in_=k_scales[0].bitcast(I32))
+        nc.sync.dma_start(out=cs_all[C_ROW:P:8, :], in_=c_scales[0].bitcast(I32))
         nc.sync.dma_start(out=q_raw[:, 2:4, :], in_=q_rows[:, 2:4, :])
         kw_all = pool.tile([P, T], I32, name="kw_all")
         nc.sync.dma_start(out=kw_all[:], in_=k_words[0].rearrange("p t r -> p (t r)").bitcast(I32))
-        for r in range(4):
-            nc.sync.dma_start(out=cs_all[C_ROW + r:P:32, :], in_=cs_rows[r:16:4, :])
         cw_all = pool.tile([P, T], I32, name="cw_all")
         nc.sync.dma_start(out=cw_all[:], in_=c_words[0].rearrange("p t r -> p (t r)").bitcast(I32))
 
+        ks = pool.tile([P, N // 4], I32, name="ks", align_bytes=64)
+        nc.gpsimd.memset(ks[:], 0)
+
         q_grouped = pool.tile([P, NQ, PACK], BF16, name="q_grouped", align_bytes=64)
-        for j in (0, 2):
+
+        def cast(j):
             nc.scalar.copy(out=q_grouped[:, :, j:j + 2].rearrange("p (c i) j -> p c j i", i=4),
                            in_=q_raw[:, j:j + 2, :].rearrange("p j (c i) -> p c j i", i=4))
 
-        ks = pool.tile([P, N], U8, name="ks", align_bytes=64)
-        nc.vector.tensor_copy(ks[:], ks_all[:].bitcast(U8).indirect(offsets[:]))
+        cast(0)
+        cast(2)
+        ks_got = pool.tile([P, N], U8, name="ks_got")
+        nc.vector.tensor_copy(ks_got[:], ks_all[:].bitcast(U8).indirect(offsets[:]))
+        for r in range(4):
+            nc.scalar.dma_start(out=ks[r:P:32, :], in_=ks_got[8 * r:P:32, :].bitcast(I32))
+        cs_got = pool.tile([P, N], U8, name="cs_got")
+        nc.vector.tensor_copy(cs_got[:], cs_all[:].bitcast(U8).indirect(offsets[:]))
 
         q_codes = pool.tile([P, NQ], U32, name="q_codes", align_bytes=64)
         q_scales = pool.tile([P, NQ], U8, name="q_scales", align_bytes=64)
         nc.vector.quantize_mx(out=q_codes[:].bitcast(FP8X4), scales=q_scales[:],
                               in_=q_grouped[:].rearrange("p w j -> p (w j)"))
+        cs = pool.tile([P, N // 4], I32, name="cs", align_bytes=64)
+        nc.vector.tensor_copy(cs[:], cs_got[:].bitcast(I32))
+        for r in range(1, 4):
+            nc.sync.dma_start(out=cs[C_ROW + r:P:32, :], in_=cs_got[C_ROW + 8 * r:P:32, :].bitcast(I32))
 
         kw = pool.tile([P, N], U32, name="kw", align_bytes=64)
         nc.vector.tensor_copy(kw[:], kw_all[:].bitcast(U32).indirect(offsets[:]))
-        cs = pool.tile([P, N], U8, name="cs", align_bytes=64)
-        nc.vector.tensor_copy(cs[:], cs_all[:].bitcast(U8).indirect(offsets[:]))
 
         def scores(acc, b, words, scales):
             cols = slice(b * P, (b + 1) * P)
@@ -79,7 +84,7 @@ def tile_attend_cfg_topk_kernel(tc, qT, k_words, k_scales, c_words, c_scales, of
         a_neg = pool.tile([P, 2, N], F32, name="a_neg")
         for b in range(2):
             a = psum.tile([P, N], F32, name=f"a{b}")
-            scores(a[:], b, kw[:], ks[:])
+            scores(a[:], b, kw[:], ks[:].bitcast(U8))
             nc.scalar.activation(out=a_neg[:, b, :], in_=a[:], func=ACT.Copy, scale=-1.5)
 
         cw = [pool.tile([P, HALF], U32, name=f"cw{h}", align_bytes=64) for h in range(2)]
@@ -87,17 +92,13 @@ def tile_attend_cfg_topk_kernel(tc, qT, k_words, k_scales, c_words, c_scales, of
             nc.vector.tensor_copy(cw[h][:], cw_all[:].bitcast(U32).indirect(offsets[:, h * 16:(h + 1) * 16]))
 
         g_neg = pool.tile([P, 2, N], F32, name="g_neg")
-        z_first = psum.tile([P, 2, HALF], F32, name="z_first")
-        for b in range(2):
-            scores(z_first[:, b, :], b, cw[0][:], cs[C_ROW:P, 0:HALF])
-        z_second = [psum.tile([P, HALF], F32, name=f"z_second{b}") for b in range(2)]
-        for b in range(2):
-            scores(z_second[b][:], b, cw[1][:], cs[C_ROW:P, HALF:N])
-        nc.vector.scalar_tensor_tensor(out=g_neg[:, :, 0:HALF], in0=z_first[:], scalar=0.5,
-                                       in1=a_neg[:, :, 0:HALF], op0=ALU.mult, op1=ALU.add)
-        for b in range(2):
-            nc.vector.scalar_tensor_tensor(out=g_neg[:, b, HALF:N], in0=z_second[b][:], scalar=0.5,
-                                           in1=a_neg[:, b, HALF:N], op0=ALU.mult, op1=ALU.add)
+        for h in range(2):
+            slots = slice(h * HALF, (h + 1) * HALF)
+            for b in range(2):
+                z = psum.tile([P, HALF], F32, name=f"z{h}{b}")
+                scores(z[:], b, cw[h][:], cs[C_ROW:P, :].bitcast(U8)[:, slots])
+                nc.vector.scalar_tensor_tensor(out=g_neg[:, b, slots], in0=z[:], scalar=0.5,
+                                               in1=a_neg[:, b, slots], op0=ALU.mult, op1=ALU.add)
 
         m_neg = [pool.tile([P, 1], F32, name=f"m_neg{b}") for b in range(2)]
         for b in range(2):

@@ -29,8 +29,7 @@ def tile_attend_cfg_topk_kernel(tc, qT, k_words, k_scales, c_words, c_scales, of
         psum = ctx.enter_context(tc.psum_pool(name="psum", bufs=1))
 
         q_raw = pool.tile([P, PACK, NQ], F32, name="q_raw")
-        q_rows = qT[0].rearrange("(p j) w -> p j w", j=PACK)
-        nc.sync.dma_start(out=q_raw[:, 0:2, :], in_=q_rows[:, 0:2, :])
+        nc.sync.dma_start(out=q_raw[:], in_=qT[0].rearrange("(p j) w -> p j w", j=PACK))
         offsets = pool.tile([P, N // 16], U16, name="offsets")
         nc.sync.dma_start(offsets[:], offs)
 
@@ -38,9 +37,8 @@ def tile_attend_cfg_topk_kernel(tc, qT, k_words, k_scales, c_words, c_scales, of
         cs_all = pool.tile([P, T // 4], I32, name="cs_all")
         nc.vector.memset(ks_all[:], 0)
         nc.vector.memset(cs_all[:], 0)
-        nc.sync.dma_start(out=ks_all[0:P:8, :], in_=k_scales[0].bitcast(I32))
+        nc.scalar.dma_start(out=ks_all[0:P:8, :], in_=k_scales[0].bitcast(I32))
         nc.sync.dma_start(out=cs_all[C_ROW:P:8, :], in_=c_scales[0].bitcast(I32))
-        nc.sync.dma_start(out=q_raw[:, 2:4, :], in_=q_rows[:, 2:4, :])
         kw_all = pool.tile([P, T], I32, name="kw_all")
         nc.sync.dma_start(out=kw_all[:], in_=k_words[0].rearrange("p t r -> p (t r)").bitcast(I32))
         cw_all = pool.tile([P, T], I32, name="cw_all")
@@ -50,13 +48,8 @@ def tile_attend_cfg_topk_kernel(tc, qT, k_words, k_scales, c_words, c_scales, of
         nc.gpsimd.memset(ks[:], 0)
 
         q_grouped = pool.tile([P, NQ, PACK], BF16, name="q_grouped", align_bytes=64)
-
-        def cast(j):
-            nc.scalar.copy(out=q_grouped[:, :, j:j + 2].rearrange("p (c i) j -> p c j i", i=4),
-                           in_=q_raw[:, j:j + 2, :].rearrange("p j (c i) -> p c j i", i=4))
-
-        cast(0)
-        cast(2)
+        nc.scalar.copy(out=q_grouped[:].rearrange("p (c i) j -> p c j i", i=4),
+                       in_=q_raw[:].rearrange("p j (c i) -> p c j i", i=4))
         ks_got = pool.tile([P, N], U8, name="ks_got")
         nc.vector.tensor_copy(ks_got[:], ks_all[:].bitcast(U8).indirect(offsets[:]))
         for r in range(4):
@@ -73,8 +66,9 @@ def tile_attend_cfg_topk_kernel(tc, qT, k_words, k_scales, c_words, c_scales, of
         for r in range(1, 4):
             nc.sync.dma_start(out=cs[C_ROW + r:P:32, :], in_=cs_got[C_ROW + 8 * r:P:32, :].bitcast(I32))
 
-        kw = pool.tile([P, N], U32, name="kw", align_bytes=64)
-        nc.vector.tensor_copy(kw[:], kw_all[:].bitcast(U32).indirect(offsets[:]))
+        kw = [pool.tile([P, HALF], U32, name=f"kw{h}", align_bytes=64) for h in range(2)]
+        for h in range(2):
+            nc.vector.tensor_copy(kw[h][:], kw_all[:].bitcast(U32).indirect(offsets[:, h * 16:(h + 1) * 16]))
 
         def scores(acc, b, words, scales):
             cols = slice(b * P, (b + 1) * P)
@@ -82,10 +76,12 @@ def tile_attend_cfg_topk_kernel(tc, qT, k_words, k_scales, c_words, c_scales, of
                                 rhs=words.bitcast(FP8X4), rhs_scale=scales, start=True, stop=True)
 
         a_neg = pool.tile([P, 2, N], F32, name="a_neg")
-        for b in range(2):
-            a = psum.tile([P, N], F32, name=f"a{b}")
-            scores(a[:], b, kw[:], ks[:].bitcast(U8))
-            nc.scalar.activation(out=a_neg[:, b, :], in_=a[:], func=ACT.Copy, scale=-1.5)
+        for h in range(2):
+            slots = slice(h * HALF, (h + 1) * HALF)
+            for b in range(2):
+                a = psum.tile([P, HALF], F32, name=f"a{h}{b}")
+                scores(a[:], b, kw[h][:], ks[:].bitcast(U8)[:, slots])
+                nc.scalar.activation(out=a_neg[:, b, slots], in_=a[:], func=ACT.Copy, scale=-1.5)
 
         cw = [pool.tile([P, HALF], U32, name=f"cw{h}", align_bytes=64) for h in range(2)]
         for h in range(2):
@@ -111,5 +107,8 @@ def tile_attend_cfg_topk_kernel(tc, qT, k_words, k_scales, c_words, c_scales, of
             nc.scalar.activation(out=e[:], in_=g_neg[:, b, :], func=ACT.Exp, bias=m_neg[b][:], scale=-1.0,
                                  accum_out=total[:])
             nc.vector.reciprocal(out=inv[:], in_=total[:])
-            nc.vector.tensor_scalar(out=y[:], in0=e[:], scalar1=inv[:], scalar2=None, op0=ALU.mult)
-            nc.sync.dma_start(out=out[0, b * P:(b + 1) * P, :], in_=y[:])
+            pieces = 1 + b
+            for u in range(pieces):
+                slots = slice(u * N // pieces, (u + 1) * N // pieces)
+                nc.vector.tensor_scalar(out=y[:, slots], in0=e[:, slots], scalar1=inv[:], scalar2=None, op0=ALU.mult)
+                nc.sync.dma_start(out=out[0, b * P:(b + 1) * P, slots], in_=y[:, slots])

@@ -42,17 +42,18 @@ def tile_attend_cfg_topk_kernel(tc, qT, k_words, k_scales, c_words, c_scales, of
         kw_all = pool.tile([P, T], I32, name="kw_all")
         nc.sync.dma_start(out=kw_all[:], in_=k_words[0].rearrange("p t r -> p (t r)").bitcast(I32))
         cw_all = pool.tile([P, T], I32, name="cw_all")
-        nc.sync.dma_start(out=cw_all[:], in_=c_words[0].rearrange("p t r -> p (t r)").bitcast(I32))
-
-        ks = pool.tile([P, N // 4], I32, name="ks", align_bytes=64)
-        nc.gpsimd.memset(ks[:], 0)
+        c_cols = c_words[0].rearrange("p t r -> p (t r)").bitcast(I32)
+        for tokens in (slice(0, 3 * T // 4), slice(3 * T // 4, T)):
+            nc.sync.dma_start(out=cw_all[:, tokens], in_=c_cols[:, tokens])
 
         q_grouped = pool.tile([P, NQ, PACK], BF16, name="q_grouped", align_bytes=64)
         nc.scalar.copy(out=q_grouped[:].rearrange("p (c i) j -> p c j i", i=4),
                        in_=q_raw[:].rearrange("p j (c i) -> p c j i", i=4))
         ks_got = pool.tile([P, N], U8, name="ks_got")
         nc.vector.tensor_copy(ks_got[:], ks_all[:].bitcast(U8).indirect(offsets[:]))
-        for r in range(4):
+        ks = pool.tile([P, N // 4], I32, name="ks", align_bytes=64)
+        nc.vector.tensor_copy(ks[:], ks_got[:].bitcast(I32))
+        for r in range(1, 4):
             nc.scalar.dma_start(out=ks[r:P:32, :], in_=ks_got[8 * r:P:32, :].bitcast(I32))
         cs_got = pool.tile([P, N], U8, name="cs_got")
         nc.vector.tensor_copy(cs_got[:], cs_all[:].bitcast(U8).indirect(offsets[:]))

@@ -37,14 +37,15 @@ def tile_attend_cfg_topk_kernel(tc, qT, k_words, k_scales, c_words, c_scales, of
         cs_all = pool.tile([P, T // 4], I32, name="cs_all")
         nc.vector.memset(ks_all[:], 0)
         nc.vector.memset(cs_all[:], 0)
-        nc.scalar.dma_start(out=ks_all[0:P:8, :], in_=k_scales[0].bitcast(I32))
-        nc.sync.dma_start(out=cs_all[C_ROW:P:8, :], in_=c_scales[0].bitcast(I32))
+        nc.sync.dma_start(out=ks_all[0:P:8, :], in_=k_scales[0].bitcast(I32))
         kw_all = pool.tile([P, T], I32, name="kw_all")
-        nc.sync.dma_start(out=kw_all[:], in_=k_words[0].rearrange("p t r -> p (t r)").bitcast(I32))
+        k_cols = k_words[0].rearrange("p t r -> p (t r)").bitcast(I32)
+        nc.sync.dma_start(out=kw_all[:, 0:T // 4], in_=k_cols[:, 0:T // 4])
+        nc.sync.dma_start(out=cs_all[C_ROW:P:8, :], in_=c_scales[0].bitcast(I32))
+        nc.sync.dma_start(out=kw_all[:, T // 4:T], in_=k_cols[:, T // 4:T])
         cw_all = pool.tile([P, T], I32, name="cw_all")
         c_cols = c_words[0].rearrange("p t r -> p (t r)").bitcast(I32)
-        for tokens in (slice(0, 3 * T // 4), slice(3 * T // 4, T)):
-            nc.sync.dma_start(out=cw_all[:, tokens], in_=c_cols[:, tokens])
+        nc.sync.dma_start(out=cw_all[:, 0:3 * T // 4], in_=c_cols[:, 0:3 * T // 4])
 
         q_grouped = pool.tile([P, NQ, PACK], BF16, name="q_grouped", align_bytes=64)
         nc.scalar.copy(out=q_grouped[:].rearrange("p (c i) j -> p c j i", i=4),
@@ -54,7 +55,8 @@ def tile_attend_cfg_topk_kernel(tc, qT, k_words, k_scales, c_words, c_scales, of
         ks = pool.tile([P, N // 4], I32, name="ks", align_bytes=64)
         nc.vector.tensor_copy(ks[:], ks_got[:].bitcast(I32))
         for r in range(1, 4):
-            nc.scalar.dma_start(out=ks[r:P:32, :], in_=ks_got[8 * r:P:32, :].bitcast(I32))
+            nc.sync.dma_start(out=ks[r:P:32, :], in_=ks_got[8 * r:P:32, :].bitcast(I32))
+        nc.sync.dma_start(out=cw_all[:, 3 * T // 4:T], in_=c_cols[:, 3 * T // 4:T])
         cs_got = pool.tile([P, N], U8, name="cs_got")
         nc.vector.tensor_copy(cs_got[:], cs_all[:].bitcast(U8).indirect(offsets[:]))
 
@@ -108,8 +110,5 @@ def tile_attend_cfg_topk_kernel(tc, qT, k_words, k_scales, c_words, c_scales, of
             nc.scalar.activation(out=e[:], in_=g_neg[:, b, :], func=ACT.Exp, bias=m_neg[b][:], scale=-1.0,
                                  accum_out=total[:])
             nc.vector.reciprocal(out=inv[:], in_=total[:])
-            pieces = 1 + b
-            for u in range(pieces):
-                slots = slice(u * N // pieces, (u + 1) * N // pieces)
-                nc.vector.tensor_scalar(out=y[:, slots], in0=e[:, slots], scalar1=inv[:], scalar2=None, op0=ALU.mult)
-                nc.sync.dma_start(out=out[0, b * P:(b + 1) * P, slots], in_=y[:, slots])
+            nc.vector.tensor_scalar(out=y[:], in0=e[:], scalar1=inv[:], scalar2=None, op0=ALU.mult)
+            nc.sync.dma_start(out=out[0, b * P:(b + 1) * P, :], in_=y[:])

@@ -20,16 +20,19 @@ P = 128
 PACK = 4
 HALF = N // 2
 C_ROW = 4
+K_CUT = 3 * T // 8
 
 
 def tile_attend_cfg_topk_kernel(tc, qT, k_words, k_scales, c_words, c_scales, offs, out):
     nc = tc.nc
     with ExitStack() as ctx:
         pool = ctx.enter_context(tc.tile_pool(name="sbuf", bufs=1))
+        staged = ctx.enter_context(tc.tile_pool(name="staged", bufs=1))
         psum = ctx.enter_context(tc.psum_pool(name="psum", bufs=1))
 
-        q_raw = pool.tile([P, PACK, NQ], F32, name="q_raw")
-        nc.sync.dma_start(out=q_raw[:], in_=qT[0].rearrange("(p j) w -> p j w", j=PACK))
+        kw_all = pool.tile([P, T], I32, name="kw_all")
+        k_cols = k_words[0].rearrange("p t r -> p (t r)").bitcast(I32)
+        nc.sync.dma_start(out=kw_all[:, 0:K_CUT], in_=k_cols[:, 0:K_CUT])
         offsets = pool.tile([P, N // 16], U16, name="offsets")
         nc.sync.dma_start(offsets[:], offs)
 
@@ -38,11 +41,10 @@ def tile_attend_cfg_topk_kernel(tc, qT, k_words, k_scales, c_words, c_scales, of
         nc.vector.memset(ks_all[:], 0)
         nc.vector.memset(cs_all[:], 0)
         nc.sync.dma_start(out=ks_all[0:P:8, :], in_=k_scales[0].bitcast(I32))
-        kw_all = pool.tile([P, T], I32, name="kw_all")
-        k_cols = k_words[0].rearrange("p t r -> p (t r)").bitcast(I32)
-        nc.sync.dma_start(out=kw_all[:, 0:T // 4], in_=k_cols[:, 0:T // 4])
+        q_raw = staged.tile([P, PACK, NQ], F32, name="q_raw", offset=0, align_bytes=64)
+        nc.sync.dma_start(out=q_raw[:], in_=qT[0].rearrange("(p j) w -> p j w", j=PACK))
         nc.sync.dma_start(out=cs_all[C_ROW:P:8, :], in_=c_scales[0].bitcast(I32))
-        nc.sync.dma_start(out=kw_all[:, T // 4:T], in_=k_cols[:, T // 4:T])
+        nc.sync.dma_start(out=kw_all[:, K_CUT:T], in_=k_cols[:, K_CUT:T])
         cw_all = pool.tile([P, T], I32, name="cw_all")
         c_cols = c_words[0].rearrange("p t r -> p (t r)").bitcast(I32)
         nc.sync.dma_start(out=cw_all[:, 0:3 * T // 4], in_=c_cols[:, 0:3 * T // 4])
@@ -64,14 +66,14 @@ def tile_attend_cfg_topk_kernel(tc, qT, k_words, k_scales, c_words, c_scales, of
         q_scales = pool.tile([P, NQ], U8, name="q_scales", align_bytes=64)
         nc.vector.quantize_mx(out=q_codes[:].bitcast(FP8X4), scales=q_scales[:],
                               in_=q_grouped[:].rearrange("p w j -> p (w j)"))
-        cs = pool.tile([P, N // 4], I32, name="cs", align_bytes=64)
+        cs = staged.tile([P, N // 4], I32, name="cs", offset=4 * N, align_bytes=64)
         nc.vector.tensor_copy(cs[:], cs_got[:].bitcast(I32))
         for r in range(1, 4):
             nc.sync.dma_start(out=cs[C_ROW + r:P:32, :], in_=cs_got[C_ROW + 8 * r:P:32, :].bitcast(I32))
 
-        kw = [pool.tile([P, HALF], U32, name=f"kw{h}", align_bytes=64) for h in range(2)]
+        kw = staged.tile([P, N], U32, name="kw", offset=0, align_bytes=64)
         for h in range(2):
-            nc.vector.tensor_copy(kw[h][:], kw_all[:].bitcast(U32).indirect(offsets[:, h * 16:(h + 1) * 16]))
+            nc.vector.tensor_copy(kw[:, h * HALF:(h + 1) * HALF], kw_all[:].bitcast(U32).indirect(offsets[:, h * 16:(h + 1) * 16]))
 
         def scores(acc, b, words, scales):
             cols = slice(b * P, (b + 1) * P)
@@ -83,7 +85,7 @@ def tile_attend_cfg_topk_kernel(tc, qT, k_words, k_scales, c_words, c_scales, of
             slots = slice(h * HALF, (h + 1) * HALF)
             for b in range(2):
                 a = psum.tile([P, HALF], F32, name=f"a{h}{b}")
-                scores(a[:], b, kw[h][:], ks[:].bitcast(U8)[:, slots])
+                scores(a[:], b, kw[:, slots], ks[:].bitcast(U8)[:, slots])
                 nc.scalar.activation(out=a_neg[:, b, slots], in_=a[:], func=ACT.Copy, scale=-1.5)
 
         cw = [pool.tile([P, HALF], U32, name=f"cw{h}", align_bytes=64) for h in range(2)]

@@ -1,6 +1,7 @@
 from contextlib import ExitStack
 
 import concourse.mybir as mybir
+from concourse.masks import make_identity
 
 N, T, D, NQ = 512, 2048, 512, 256
 FLOPS = 2 * 2 * NQ * N * D
@@ -36,7 +37,7 @@ def tile_attend_cfg_topk_kernel(tc, qT, k_words, k_scales, c_words, c_scales, of
         offsets = pool.tile([P, N // 16], U16, name="offsets")
         nc.sync.dma_start(offsets[:], offs)
 
-        ks_all = pool.tile([P, T // 4], I32, name="ks_all")
+        ks_all = pool.tile([P, T // 4], I32, name="ks_all", tag="ks_then_identity")
         cs_all = pool.tile([P, T // 4], I32, name="cs_all")
         nc.vector.memset(ks_all[:], 0)
         nc.vector.memset(cs_all[:], 0)
@@ -75,35 +76,64 @@ def tile_attend_cfg_topk_kernel(tc, qT, k_words, k_scales, c_words, c_scales, of
         for h in range(2):
             nc.vector.tensor_copy(kw[:, h * HALF:(h + 1) * HALF], kw_all[:].bitcast(U32).indirect(offsets[:, h * 16:(h + 1) * 16]))
 
-        def scores(acc, b, words, scales):
-            cols = slice(b * P, (b + 1) * P)
-            nc.tensor.matmul_mx(out=acc, lhsT=q_codes[:, cols].bitcast(FP8X4), lhsT_scale=q_scales[:, cols],
+        identity = pool.tile([P, P], F32, name="identity", tag="ks_then_identity")
+        make_identity(nc, identity[:])
+        ks_bytes = ks[:].bitcast(U8)
+        cs_bytes = cs[C_ROW:P, :].bitcast(U8)
+
+        def by_query(acc, words, scales):
+            nc.tensor.matmul_mx(out=acc, lhsT=q_codes[:, 0:P].bitcast(FP8X4), lhsT_scale=q_scales[:, 0:P],
                                 rhs=words.bitcast(FP8X4), rhs_scale=scales, start=True, stop=True)
 
-        a_neg = pool.tile([P, 2, N], F32, name="a_neg")
+        def by_slot(acc, words, scales):
+            nc.tensor.matmul_mx(out=acc, lhsT=words.bitcast(FP8X4), lhsT_scale=scales,
+                                rhs=q_codes[:, P:NQ].bitcast(FP8X4), rhs_scale=q_scales[:, P:NQ],
+                                start=True, stop=True)
+
+        def turned(h, words, scales, factor, name):
+            acc = psum.tile([P, 2, P], F32, name=f"{name}_psum{h}", tag=f"by_slot{h}")
+            for t in range(2):
+                by_slot(acc[:, t, :], words[:, t * P:(t + 1) * P], scales[:, h * HALF + t * P:h * HALF + (t + 1) * P])
+            held = pool.tile([P, 2, P], F32, name=f"{name}{h}")
+            nc.scalar.activation(out=held[:], in_=acc[:], func=ACT.Copy, scale=factor)
+            return held
+
+        a_neg = pool.tile([P, N], F32, name="a_neg")
+        a_turned = []
         for h in range(2):
             slots = slice(h * HALF, (h + 1) * HALF)
-            for b in range(2):
-                a = psum.tile([P, HALF], F32, name=f"a{h}{b}")
-                scores(a[:], b, kw[:, slots], ks[:].bitcast(U8)[:, slots])
-                nc.scalar.activation(out=a_neg[:, b, slots], in_=a[:], func=ACT.Copy, scale=-1.5)
+            a_turned.append(turned(h, kw[:, slots], ks_bytes, -1.5, "a_turned"))
+            a = psum.tile([P, HALF], F32, name=f"a{h}")
+            by_query(a[:], kw[:, slots], ks_bytes[:, slots])
+            nc.scalar.activation(out=a_neg[:, slots], in_=a[:], func=ACT.Copy, scale=-1.5)
 
         cw = [pool.tile([P, HALF], U32, name=f"cw{h}", align_bytes=64) for h in range(2)]
         for h in range(2):
             nc.vector.tensor_copy(cw[h][:], cw_all[:].bitcast(U32).indirect(offsets[:, h * 16:(h + 1) * 16]))
 
         g_neg = pool.tile([P, 2, N], F32, name="g_neg")
+        z_turned = []
         for h in range(2):
             slots = slice(h * HALF, (h + 1) * HALF)
-            for b in range(2):
-                z = psum.tile([P, HALF], F32, name=f"z{h}{b}")
-                scores(z[:], b, cw[h][:], cs[C_ROW:P, :].bitcast(U8)[:, slots])
-                nc.vector.scalar_tensor_tensor(out=g_neg[:, b, slots], in0=z[:], scalar=0.5,
-                                               in1=a_neg[:, b, slots], op0=ALU.mult, op1=ALU.add)
+            z = psum.tile([P, HALF], F32, name=f"z{h}", tag=f"z_then_g{h}")
+            by_query(z[:], cw[h][:], cs_bytes[:, slots])
+            nc.vector.scalar_tensor_tensor(out=g_neg[:, 0, slots], in0=z[:], scalar=0.5,
+                                           in1=a_neg[:, slots], op0=ALU.mult, op1=ALU.add)
+            z_turned.append(turned(h, cw[h], cs_bytes, 0.5, "z_turned"))
+        g_psum = [psum.tile([P, 2, P], F32, name=f"g_psum{h}", tag=("z_then_g0", "by_slot0")[h]) for h in range(2)]
+        for h in range(2):
+            for i, held in enumerate((a_turned[h], z_turned[h])):
+                for t in range(2):
+                    nc.tensor.matmul(g_psum[h][:, t, :], lhsT=held[:, t, :], rhs=identity[:], is_transpose=True,
+                                     start=(i == 0 and t == 0), stop=(i == 1 and t == 1))
 
         m_neg = [pool.tile([P, 1], F32, name=f"m_neg{b}") for b in range(2)]
-        for b in range(2):
-            nc.vector.tensor_reduce(out=m_neg[b][:], in_=g_neg[:, b, :], axis=AX.X, op=ALU.min)
+        nc.vector.tensor_reduce(out=m_neg[0][:], in_=g_neg[:, 0, :], axis=AX.X, op=ALU.min)
+        m_half = pool.tile([P, 1], F32, name="m_half")
+        nc.vector.tensor_scalar(out=g_neg[:, 1, 0:HALF], in0=g_psum[0][:].rearrange("p t s -> p (t s)"), scalar1=1.0,
+                                scalar2=None, op0=ALU.mult, op1=ALU.min, accum_out=m_half[:])
+        nc.vector.tensor_scalar(out=g_neg[:, 1, HALF:N], in0=g_psum[1][:].rearrange("p t s -> p (t s)"), scalar1=1.0,
+                                scalar2=m_half[:], op0=ALU.mult, op1=ALU.min, accum_out=m_neg[1][:])
         for b in range(2):
             e = pool.tile([P, N], F32, name=f"e{b}")
             total = pool.tile([P, 1], F32, name=f"total{b}")

@@ -98,6 +98,11 @@ def tile_attend_cfg_topk_kernel(tc, qT, k_words, k_scales, c_words, c_scales, of
             nc.scalar.activation(out=held[:], in_=acc[:], func=ACT.Copy, scale=factor)
             return held
 
+        def add_turned(g_turned, h, held, first, last):
+            for t in range(2):
+                nc.tensor.matmul(g_turned[:, 2 * h + t, :], lhsT=held[:, t, :], rhs=identity[:], is_transpose=True,
+                                 start=(first and t == 0), stop=(last and t == 1))
+
         a_neg = pool.tile([P, N], F32, name="a_neg")
         a_turned = []
         for h in range(2):
@@ -111,35 +116,34 @@ def tile_attend_cfg_topk_kernel(tc, qT, k_words, k_scales, c_words, c_scales, of
         for h in range(2):
             nc.vector.tensor_copy(cw[h][:], cw_all[:].bitcast(U32).indirect(offsets[:, h * 16:(h + 1) * 16]))
 
-        g_neg = pool.tile([P, 2, N], F32, name="g_neg")
+        g_first = pool.tile([P, N], F32, name="g_first")
+        g_late = pool.tile([P, HALF], F32, name="g_late")
+        m_half = pool.tile([P, 1], F32, name="m_half")
         z_turned = []
         for h in range(2):
             slots = slice(h * HALF, (h + 1) * HALF)
-            z = psum.tile([P, HALF], F32, name=f"z{h}", tag=f"z_then_g{h}")
+            z = psum.tile([P, HALF], F32, name=f"z{h}", tag=f"z{h}")
             by_query(z[:], cw[h][:], cs_bytes[:, slots])
-            nc.vector.scalar_tensor_tensor(out=g_neg[:, 0, slots], in0=z[:], scalar=0.5,
+            nc.vector.scalar_tensor_tensor(out=(g_first[:, slots], g_late[:])[h], in0=z[:], scalar=0.5,
                                            in1=a_neg[:, slots], op0=ALU.mult, op1=ALU.add)
+            if h == 0:
+                nc.vector.tensor_reduce(out=m_half[:], in_=g_first[:, slots], axis=AX.X, op=ALU.min)
             z_turned.append(turned(h, cw[h], cs_bytes, 0.5, "z_turned"))
-        g_psum = [psum.tile([P, 2, P], F32, name=f"g_psum{h}", tag=("z_then_g0", "by_slot0")[h]) for h in range(2)]
-        for h in range(2):
-            for i, held in enumerate((a_turned[h], z_turned[h])):
-                for t in range(2):
-                    nc.tensor.matmul(g_psum[h][:, t, :], lhsT=held[:, t, :], rhs=identity[:], is_transpose=True,
-                                     start=(i == 0 and t == 0), stop=(i == 1 and t == 1))
+        g_turned = psum.tile([P, 4, P], F32, name="g_turned", tag="z0")
+        for i, (h, held) in enumerate(((0, a_turned[0]), (1, a_turned[1]), (0, z_turned[0]), (1, z_turned[1]))):
+            add_turned(g_turned, h, held, i == 0, i == 3)
 
+        g_neg = (g_first[:], g_turned[:].rearrange("p t s -> p (t s)"))
         m_neg = [pool.tile([P, 1], F32, name=f"m_neg{b}") for b in range(2)]
-        nc.vector.tensor_reduce(out=m_neg[0][:], in_=g_neg[:, 0, :], axis=AX.X, op=ALU.min)
-        m_half = pool.tile([P, 1], F32, name="m_half")
-        nc.vector.tensor_scalar(out=g_neg[:, 1, 0:HALF], in0=g_psum[0][:].rearrange("p t s -> p (t s)"), scalar1=1.0,
-                                scalar2=None, op0=ALU.mult, op1=ALU.min, accum_out=m_half[:])
-        nc.vector.tensor_scalar(out=g_neg[:, 1, HALF:N], in0=g_psum[1][:].rearrange("p t s -> p (t s)"), scalar1=1.0,
-                                scalar2=m_half[:], op0=ALU.mult, op1=ALU.min, accum_out=m_neg[1][:])
+        nc.vector.tensor_scalar(out=g_first[:, HALF:N], in0=g_late[:], scalar1=1.0, scalar2=m_half[:],
+                                op0=ALU.mult, op1=ALU.min, accum_out=m_neg[0][:])
+        nc.vector.tensor_reduce(out=m_neg[1][:], in_=g_neg[1], axis=AX.X, op=ALU.min)
         for b in range(2):
             e = pool.tile([P, N], F32, name=f"e{b}")
             total = pool.tile([P, 1], F32, name=f"total{b}")
             inv = pool.tile([P, 1], F32, name=f"inv{b}")
             y = pool.tile([P, N], F32, name=f"y{b}")
-            nc.scalar.activation(out=e[:], in_=g_neg[:, b, :], func=ACT.Exp, bias=m_neg[b][:], scale=-1.0,
+            nc.scalar.activation(out=e[:], in_=g_neg[b], func=ACT.Exp, bias=m_neg[b][:], scale=-1.0,
                                  accum_out=total[:])
             nc.vector.reciprocal(out=inv[:], in_=total[:])
             nc.vector.tensor_scalar(out=y[:], in0=e[:], scalar1=inv[:], scalar2=None, op0=ALU.mult)

@@ -90,6 +90,12 @@ def tile_attend_cfg_topk_kernel(tc, qT, k_words, k_scales, c_words, c_scales, of
                                 rhs=q_codes[:, P:NQ].bitcast(FP8X4), rhs_scale=q_scales[:, P:NQ],
                                 start=True, stop=True)
 
+        warm = psum.tile([P, 2, NQ], F32, name="warm")
+        for b in range(2):
+            cols = slice(b * P, (b + 1) * P)
+            nc.tensor.matmul_mx(out=warm[:, b, :], lhsT=q_codes[:, cols].bitcast(FP8X4), lhsT_scale=q_scales[:, cols],
+                                rhs=q_codes[:].bitcast(FP8X4), rhs_scale=q_scales[:], start=True, stop=True)
+
         def turned(h, words, scales, factor, name):
             acc = psum.tile([P, 2, P], F32, name=f"{name}_psum{h}", tag=f"by_slot{h}")
             for t in range(2):

@@ -90,7 +90,7 @@ def tile_attend_cfg_topk_kernel(tc, qT, k_words, k_scales, c_words, c_scales, of
                                 rhs=q_codes[:, P:NQ].bitcast(FP8X4), rhs_scale=q_scales[:, P:NQ],
                                 start=True, stop=True)
 
-        warm = psum.tile([P, 2, NQ], F32, name="warm")
+        warm = psum.tile([P, 2, NQ], F32, name="warm", tag="warm")
         for b in range(2):
             cols = slice(b * P, (b + 1) * P)
             nc.tensor.matmul_mx(out=warm[:, b, :], lhsT=q_codes[:, cols].bitcast(FP8X4), lhsT_scale=q_scales[:, cols],
@@ -102,6 +102,14 @@ def tile_attend_cfg_topk_kernel(tc, qT, k_words, k_scales, c_words, c_scales, of
                 by_slot(acc[:, t, :], words[:, t * P:(t + 1) * P], scales[:, h * HALF + t * P:h * HALF + (t + 1) * P])
             held = pool.tile([P, 2, P], F32, name=f"{name}{h}")
             nc.scalar.activation(out=held[:], in_=acc[:], func=ACT.Copy, scale=factor)
+            return held
+
+        def turned_by_tile(h, words, scales, factor, name, tags):
+            held = pool.tile([P, 2, P], F32, name=f"{name}{h}")
+            for t in range(2):
+                acc = psum.tile([P, P], F32, name=f"{name}_psum{h}{t}", tag=tags[t])
+                by_slot(acc[:], words[:, t * P:(t + 1) * P], scales[:, h * HALF + t * P:h * HALF + (t + 1) * P])
+                nc.scalar.activation(out=held[:, t, :], in_=acc[:], func=ACT.Copy, scale=factor)
             return held
 
         def add_turned(g_turned, h, held, first, last):
@@ -123,27 +131,25 @@ def tile_attend_cfg_topk_kernel(tc, qT, k_words, k_scales, c_words, c_scales, of
             nc.vector.tensor_copy(cw[h][:], cw_all[:].bitcast(U32).indirect(offsets[:, h * 16:(h + 1) * 16]))
 
         g_first = pool.tile([P, N], F32, name="g_first")
-        g_late = pool.tile([P, HALF], F32, name="g_late")
-        m_half = pool.tile([P, 1], F32, name="m_half")
         z_turned = []
         for h in range(2):
             slots = slice(h * HALF, (h + 1) * HALF)
             z = psum.tile([P, HALF], F32, name=f"z{h}", tag=f"z{h}")
             by_query(z[:], cw[h][:], cs_bytes[:, slots])
-            nc.vector.scalar_tensor_tensor(out=(g_first[:, slots], g_late[:])[h], in0=z[:], scalar=0.5,
+            nc.vector.scalar_tensor_tensor(out=g_first[:, slots], in0=z[:], scalar=0.5,
                                            in1=a_neg[:, slots], op0=ALU.mult, op1=ALU.add)
             if h == 0:
-                nc.vector.tensor_reduce(out=m_half[:], in_=g_first[:, slots], axis=AX.X, op=ALU.min)
-            z_turned.append(turned(h, cw[h], cs_bytes, 0.5, "z_turned"))
+                z_turned.append(turned(h, cw[h], cs_bytes, 0.5, "z_turned"))
+            else:
+                z_turned.append(turned_by_tile(h, cw[h], cs_bytes, 0.5, "z_turned", ("by_slot1", "warm")))
         g_turned = psum.tile([P, 4, P], F32, name="g_turned", tag="z0")
         for i, (h, held) in enumerate(((0, a_turned[0]), (1, a_turned[1]), (0, z_turned[0]), (1, z_turned[1]))):
             add_turned(g_turned, h, held, i == 0, i == 3)
 
         g_neg = (g_first[:], g_turned[:].rearrange("p t s -> p (t s)"))
         m_neg = [pool.tile([P, 1], F32, name=f"m_neg{b}") for b in range(2)]
-        nc.vector.tensor_scalar(out=g_first[:, HALF:N], in0=g_late[:], scalar1=1.0, scalar2=m_half[:],
-                                op0=ALU.mult, op1=ALU.min, accum_out=m_neg[0][:])
-        nc.vector.tensor_reduce(out=m_neg[1][:], in_=g_neg[1], axis=AX.X, op=ALU.min)
+        for b in range(2):
+            nc.vector.tensor_reduce(out=m_neg[b][:], in_=g_neg[b], axis=AX.X, op=ALU.min)
         for b in range(2):
             e = pool.tile([P, N], F32, name=f"e{b}")
             total = pool.tile([P, 1], F32, name=f"total{b}")

@@ -21,7 +21,7 @@ P = 128
 PACK = 4
 HALF = N // 2
 C_ROW = 4
-K_CUT = 3 * T // 8
+C_CUT = 13 * T // 16
 
 
 def tile_attend_cfg_topk_kernel(tc, qT, k_words, k_scales, c_words, c_scales, offs, out):
@@ -31,9 +31,8 @@ def tile_attend_cfg_topk_kernel(tc, qT, k_words, k_scales, c_words, c_scales, of
         staged = ctx.enter_context(tc.tile_pool(name="staged", bufs=1))
         psum = ctx.enter_context(tc.psum_pool(name="psum", bufs=1))
 
-        kw_all = pool.tile([P, T], I32, name="kw_all")
-        k_cols = k_words[0].rearrange("p t r -> p (t r)").bitcast(I32)
-        nc.sync.dma_start(out=kw_all[:, 0:K_CUT], in_=k_cols[:, 0:K_CUT])
+        q_raw = staged.tile([P, PACK, NQ], F32, name="q_raw", offset=0, align_bytes=64)
+        nc.sync.dma_start(out=q_raw[:], in_=qT[0].rearrange("(p j) w -> p j w", j=PACK))
         offsets = pool.tile([P, N // 16], U16, name="offsets")
         nc.sync.dma_start(offsets[:], offs)
 
@@ -42,13 +41,12 @@ def tile_attend_cfg_topk_kernel(tc, qT, k_words, k_scales, c_words, c_scales, of
         nc.vector.memset(ks_all[:], 0)
         nc.vector.memset(cs_all[:], 0)
         nc.sync.dma_start(out=ks_all[0:P:8, :], in_=k_scales[0].bitcast(I32))
-        q_raw = staged.tile([P, PACK, NQ], F32, name="q_raw", offset=0, align_bytes=64)
-        nc.sync.dma_start(out=q_raw[:], in_=qT[0].rearrange("(p j) w -> p j w", j=PACK))
         nc.sync.dma_start(out=cs_all[C_ROW:P:8, :], in_=c_scales[0].bitcast(I32))
-        nc.sync.dma_start(out=kw_all[:, K_CUT:T], in_=k_cols[:, K_CUT:T])
+        kw_all = pool.tile([P, T], I32, name="kw_all")
+        nc.sync.dma_start(out=kw_all[:], in_=k_words[0].rearrange("p t r -> p (t r)").bitcast(I32))
         cw_all = pool.tile([P, T], I32, name="cw_all")
         c_cols = c_words[0].rearrange("p t r -> p (t r)").bitcast(I32)
-        nc.sync.dma_start(out=cw_all[:, 0:3 * T // 4], in_=c_cols[:, 0:3 * T // 4])
+        nc.sync.dma_start(out=cw_all[:, 0:C_CUT], in_=c_cols[:, 0:C_CUT])
 
         q_grouped = pool.tile([P, NQ, PACK], BF16, name="q_grouped", align_bytes=64)
         nc.scalar.copy(out=q_grouped[:].rearrange("p (c i) j -> p c j i", i=4),
@@ -59,7 +57,7 @@ def tile_attend_cfg_topk_kernel(tc, qT, k_words, k_scales, c_words, c_scales, of
         nc.vector.tensor_copy(ks[:], ks_got[:].bitcast(I32))
         for r in range(1, 4):
             nc.sync.dma_start(out=ks[r:P:32, :], in_=ks_got[8 * r:P:32, :].bitcast(I32))
-        nc.sync.dma_start(out=cw_all[:, 3 * T // 4:T], in_=c_cols[:, 3 * T // 4:T])
+        nc.sync.dma_start(out=cw_all[:, C_CUT:T], in_=c_cols[:, C_CUT:T])
         cs_got = pool.tile([P, N], U8, name="cs_got")
         nc.vector.tensor_copy(cs_got[:], cs_all[:].bitcast(U8).indirect(offsets[:]))
 
@@ -158,5 +156,6 @@ def tile_attend_cfg_topk_kernel(tc, qT, k_words, k_scales, c_words, c_scales, of
             nc.scalar.activation(out=e[:], in_=g_neg[b], func=ACT.Exp, bias=m_neg[b][:], scale=-1.0,
                                  accum_out=total[:])
             nc.vector.reciprocal(out=inv[:], in_=total[:])
-            nc.vector.tensor_scalar(out=y[:], in0=e[:], scalar1=inv[:], scalar2=None, op0=ALU.mult)
-            nc.sync.dma_start(out=out[0, b * P:(b + 1) * P, :], in_=y[:])
+            for slots in ((slice(0, N),), (slice(0, HALF), slice(HALF, N)))[b]:
+                nc.vector.tensor_scalar(out=y[:, slots], in0=e[:, slots], scalar1=inv[:], scalar2=None, op0=ALU.mult)
+                nc.sync.dma_start(out=out[0, b * P:(b + 1) * P, slots], in_=y[:, slots])

@@ -21,7 +21,7 @@ P = 128
 PACK = 4
 HALF = N // 2
 C_ROW = 4
-C_CUT = 13 * T // 16
+C_CUT = 7 * T // 8
 
 
 def tile_attend_cfg_topk_kernel(tc, qT, k_words, k_scales, c_words, c_scales, offs, out):

@@ -67,8 +67,8 @@ def tile_attend_cfg_topk_kernel(tc, qT, k_words, k_scales, c_words, c_scales, of
                               in_=q_grouped[:].rearrange("p w j -> p (w j)"))
         cs = staged.tile([P, N // 4], I32, name="cs", offset=4 * N, align_bytes=64)
         nc.vector.tensor_copy(cs[:], cs_got[:].bitcast(I32))
-        for r in range(1, 4):
-            nc.sync.dma_start(out=cs[C_ROW + r:P:32, :], in_=cs_got[C_ROW + 8 * r:P:32, :].bitcast(I32))
+        for r, queue in ((1, nc.sync), (2, nc.scalar), (3, nc.sync)):
+            queue.dma_start(out=cs[C_ROW + r:P:32, :], in_=cs_got[C_ROW + 8 * r:P:32, :].bitcast(I32))
 
         kw = staged.tile([P, N], U32, name="kw", offset=0, align_bytes=64)
         for h in range(2):

@@ -88,12 +88,6 @@ def tile_attend_cfg_topk_kernel(tc, qT, k_words, k_scales, c_words, c_scales, of
                                 rhs=q_codes[:, P:NQ].bitcast(FP8X4), rhs_scale=q_scales[:, P:NQ],
                                 start=True, stop=True)
 
-        warm = psum.tile([P, 2, NQ], F32, name="warm", tag="warm")
-        for b in range(2):
-            cols = slice(b * P, (b + 1) * P)
-            nc.tensor.matmul_mx(out=warm[:, b, :], lhsT=q_codes[:, cols].bitcast(FP8X4), lhsT_scale=q_scales[:, cols],
-                                rhs=q_codes[:].bitcast(FP8X4), rhs_scale=q_scales[:], start=True, stop=True)
-
         def turned(h, words, scales, factor, name):
             acc = psum.tile([P, 2, P], F32, name=f"{name}_psum{h}", tag=f"by_slot{h}")
             for t in range(2):
@@ -139,7 +133,7 @@ def tile_attend_cfg_topk_kernel(tc, qT, k_words, k_scales, c_words, c_scales, of
             if h == 0:
                 z_turned.append(turned(h, cw[h], cs_bytes, 0.5, "z_turned"))
             else:
-                z_turned.append(turned_by_tile(h, cw[h], cs_bytes, 0.5, "z_turned", ("by_slot1", "warm")))
+                z_turned.append(turned_by_tile(h, cw[h], cs_bytes, 0.5, "z_turned", ("by_slot1", "by_slot2")))
         g_turned = psum.tile([P, 4, P], F32, name="g_turned", tag="z0")
         for i, (h, held) in enumerate(((0, a_turned[0]), (1, a_turned[1]), (0, z_turned[0]), (1, z_turned[1]))):
             add_turned(g_turned, h, held, i == 0, i == 3)

@@ -1,7 +1,6 @@
 from contextlib import ExitStack
 
 import concourse.mybir as mybir
-from concourse.masks import make_identity
 
 N, T, D, NQ = 512, 2048, 512, 256
 FLOPS = 2 * 2 * NQ * N * D
@@ -21,7 +20,9 @@ P = 128
 PACK = 4
 HALF = N // 2
 C_ROW = 4
-C_CUT = 7 * T // 8
+C_CUT = 3 * T // 4
+HALVES = (slice(0, HALF), slice(HALF, N))
+PIECES = (slice(0, HALF), slice(HALF, HALF + P), slice(HALF + P, N))
 
 
 def tile_attend_cfg_topk_kernel(tc, qT, k_words, k_scales, c_words, c_scales, offs, out):
@@ -36,7 +37,7 @@ def tile_attend_cfg_topk_kernel(tc, qT, k_words, k_scales, c_words, c_scales, of
         offsets = pool.tile([P, N // 16], U16, name="offsets")
         nc.sync.dma_start(offsets[:], offs)
 
-        ks_all = pool.tile([P, T // 4], I32, name="ks_all", tag="ks_then_identity")
+        ks_all = pool.tile([P, T // 4], I32, name="ks_all")
         cs_all = pool.tile([P, T // 4], I32, name="cs_all")
         nc.vector.memset(ks_all[:], 0)
         nc.vector.memset(cs_all[:], 0)
@@ -74,80 +75,51 @@ def tile_attend_cfg_topk_kernel(tc, qT, k_words, k_scales, c_words, c_scales, of
         for h in range(2):
             nc.vector.tensor_copy(kw[:, h * HALF:(h + 1) * HALF], kw_all[:].bitcast(U32).indirect(offsets[:, h * 16:(h + 1) * 16]))
 
-        identity = pool.tile([P, P], F32, name="identity", tag="ks_then_identity")
-        make_identity(nc, identity[:])
         ks_bytes = ks[:].bitcast(U8)
         cs_bytes = cs[C_ROW:P, :].bitcast(U8)
 
-        def by_query(acc, words, scales):
-            nc.tensor.matmul_mx(out=acc, lhsT=q_codes[:, 0:P].bitcast(FP8X4), lhsT_scale=q_scales[:, 0:P],
-                                rhs=words.bitcast(FP8X4), rhs_scale=scales, start=True, stop=True)
+        def scores(name, tag, b, words, scales, slots):
+            acc = psum.tile([P, slots.stop - slots.start], F32, name=name, tag=tag)
+            nc.tensor.matmul_mx(out=acc[:], lhsT=q_codes[:, b * P:(b + 1) * P].bitcast(FP8X4),
+                                lhsT_scale=q_scales[:, b * P:(b + 1) * P],
+                                rhs=words[:, slots].bitcast(FP8X4), rhs_scale=scales[:, slots], start=True, stop=True)
+            return acc
 
-        def by_slot(acc, words, scales):
-            nc.tensor.matmul_mx(out=acc, lhsT=words.bitcast(FP8X4), lhsT_scale=scales,
-                                rhs=q_codes[:, P:NQ].bitcast(FP8X4), rhs_scale=q_scales[:, P:NQ],
-                                start=True, stop=True)
-
-        def turned(h, words, scales, factor, name):
-            acc = psum.tile([P, 2, P], F32, name=f"{name}_psum{h}", tag=f"by_slot{h}")
-            for t in range(2):
-                by_slot(acc[:, t, :], words[:, t * P:(t + 1) * P], scales[:, h * HALF + t * P:h * HALF + (t + 1) * P])
-            held = pool.tile([P, 2, P], F32, name=f"{name}{h}")
-            nc.scalar.activation(out=held[:], in_=acc[:], func=ACT.Copy, scale=factor)
-            return held
-
-        def turned_by_tile(h, words, scales, factor, name, tags):
-            held = pool.tile([P, 2, P], F32, name=f"{name}{h}")
-            for t in range(2):
-                acc = psum.tile([P, P], F32, name=f"{name}_psum{h}{t}", tag=tags[t])
-                by_slot(acc[:], words[:, t * P:(t + 1) * P], scales[:, h * HALF + t * P:h * HALF + (t + 1) * P])
-                nc.scalar.activation(out=held[:, t, :], in_=acc[:], func=ACT.Copy, scale=factor)
-            return held
-
-        def add_turned(g_turned, h, held, first, last):
-            for t in range(2):
-                nc.tensor.matmul(g_turned[:, 2 * h + t, :], lhsT=held[:, t, :], rhs=identity[:], is_transpose=True,
-                                 start=(first and t == 0), stop=(last and t == 1))
-
-        a_neg = pool.tile([P, N], F32, name="a_neg")
-        a_turned = []
+        a_neg = [pool.tile([P, N], F32, name=f"a_neg{b}") for b in range(2)]
         for h in range(2):
-            slots = slice(h * HALF, (h + 1) * HALF)
-            a_turned.append(turned(h, kw[:, slots], ks_bytes, -1.5, "a_turned"))
-            a = psum.tile([P, HALF], F32, name=f"a{h}")
-            by_query(a[:], kw[:, slots], ks_bytes[:, slots])
-            nc.scalar.activation(out=a_neg[:, slots], in_=a[:], func=ACT.Copy, scale=-1.5)
+            for b in range(2):
+                a = scores(f"a{b}{h}", f"a{b}{h}", b, kw, ks_bytes, HALVES[h])
+                nc.scalar.activation(out=a_neg[b][:, HALVES[h]], in_=a[:], func=ACT.Copy, scale=-1.5)
 
-        cw = [pool.tile([P, HALF], U32, name=f"cw{h}", align_bytes=64) for h in range(2)]
-        for h in range(2):
-            nc.vector.tensor_copy(cw[h][:], cw_all[:].bitcast(U32).indirect(offsets[:, h * 16:(h + 1) * 16]))
+        cw = pool.tile([P, N], U32, name="cw", align_bytes=64)
+        for slots in PIECES:
+            nc.vector.tensor_copy(cw[:, slots], cw_all[:].bitcast(U32).indirect(offsets[:, slots.start // 16:slots.stop // 16]))
 
-        g_first = pool.tile([P, N], F32, name="g_first")
-        z_turned = []
-        for h in range(2):
-            slots = slice(h * HALF, (h + 1) * HALF)
-            z = psum.tile([P, HALF], F32, name=f"z{h}", tag=f"z{h}")
-            by_query(z[:], cw[h][:], cs_bytes[:, slots])
-            nc.vector.scalar_tensor_tensor(out=g_first[:, slots], in0=z[:], scalar=0.5,
-                                           in1=a_neg[:, slots], op0=ALU.mult, op1=ALU.add)
-            if h == 0:
-                z_turned.append(turned(h, cw[h], cs_bytes, 0.5, "z_turned"))
-            else:
-                z_turned.append(turned_by_tile(h, cw[h], cs_bytes, 0.5, "z_turned", ("by_slot1", "by_slot2")))
-        g_turned = psum.tile([P, 4, P], F32, name="g_turned", tag="z0")
-        for i, (h, held) in enumerate(((0, a_turned[0]), (1, a_turned[1]), (0, z_turned[0]), (1, z_turned[1]))):
-            add_turned(g_turned, h, held, i == 0, i == 3)
+        g_neg = [pool.tile([P, N], F32, name=f"g_neg{b}") for b in range(2)]
 
-        g_neg = (g_first[:], g_turned[:].rearrange("p t s -> p (t s)"))
+        def combine(b, slots, tag):
+            z = scores(f"z{b}_{slots.start}", tag, b, cw, cs_bytes, slots)
+            nc.vector.scalar_tensor_tensor(out=g_neg[b][:, slots], in0=z[:], scalar=0.5,
+                                           in1=a_neg[b][:, slots], op0=ALU.mult, op1=ALU.add)
+
+        combine(0, PIECES[0], "z00")
+        z = scores("z1_0", "z10", 1, cw, cs_bytes, HALVES[0])
+        z_half = pool.tile([P, HALF], F32, name="z_half")
+        nc.scalar.activation(out=z_half[:], in_=z[:], func=ACT.Copy, scale=0.5)
+        nc.gpsimd.tensor_tensor(out=g_neg[1][:, HALVES[0]], in0=z_half[:], in1=a_neg[1][:, HALVES[0]], op=ALU.add)
+        combine(0, PIECES[1], "z01")
+        combine(0, PIECES[2], "z02")
+        combine(1, HALVES[1], "a00")
+
         m_neg = [pool.tile([P, 1], F32, name=f"m_neg{b}") for b in range(2)]
         for b in range(2):
-            nc.vector.tensor_reduce(out=m_neg[b][:], in_=g_neg[b], axis=AX.X, op=ALU.min)
+            nc.vector.tensor_reduce(out=m_neg[b][:], in_=g_neg[b][:], axis=AX.X, op=ALU.min)
         for b in range(2):
             e = pool.tile([P, N], F32, name=f"e{b}")
             total = pool.tile([P, 1], F32, name=f"total{b}")
             inv = pool.tile([P, 1], F32, name=f"inv{b}")
             y = pool.tile([P, N], F32, name=f"y{b}")
-            nc.scalar.activation(out=e[:], in_=g_neg[b], func=ACT.Exp, bias=m_neg[b][:], scale=-1.0,
+            nc.scalar.activation(out=e[:], in_=g_neg[b][:], func=ACT.Exp, bias=m_neg[b][:], scale=-1.0,
                                  accum_out=total[:])
             nc.vector.reciprocal(out=inv[:], in_=total[:])
             for slots in ((slice(0, N),), (slice(0, HALF), slice(HALF, N)))[b]:

from contextlib import ExitStack

import concourse.mybir as mybir

N, T, D, NQ = 512, 2048, 512, 256
FLOPS = 2 * 2 * NQ * N * D

F32 = mybir.dt.float32
BF16 = mybir.dt.bfloat16
I32 = mybir.dt.int32
U32 = mybir.dt.uint32
U16 = mybir.dt.uint16
U8 = mybir.dt.uint8
FP8X4 = mybir.dt.float8_e4m3fn_x4
ALU = mybir.AluOpType
ACT = mybir.ActivationFunctionType
AX = mybir.AxisListType

P = 128
PACK = 4
HALF = N // 2
C_ROW = 4
C_CUT = 3 * T // 4
HALVES = (slice(0, HALF), slice(HALF, N))
PIECES = (slice(0, HALF), slice(HALF, HALF + P), slice(HALF + P, N))


def tile_attend_cfg_topk_kernel(tc, qT, k_words, k_scales, c_words, c_scales, offs, out):
    nc = tc.nc
    with ExitStack() as ctx:
        pool = ctx.enter_context(tc.tile_pool(name="sbuf", bufs=1))
        staged = ctx.enter_context(tc.tile_pool(name="staged", bufs=1))
        psum = ctx.enter_context(tc.psum_pool(name="psum", bufs=1))

        q_raw = staged.tile([P, PACK, NQ], F32, name="q_raw", offset=0, align_bytes=64)
        nc.sync.dma_start(out=q_raw[:], in_=qT[0].rearrange("(p j) w -> p j w", j=PACK))
        offsets = pool.tile([P, N // 16], U16, name="offsets")
        nc.sync.dma_start(offsets[:], offs)

        ks_all = pool.tile([P, T // 4], I32, name="ks_all")
        cs_all = pool.tile([P, T // 4], I32, name="cs_all")
        nc.vector.memset(ks_all[:], 0)
        nc.vector.memset(cs_all[:], 0)
        nc.sync.dma_start(out=ks_all[0:P:8, :], in_=k_scales[0].bitcast(I32))
        nc.sync.dma_start(out=cs_all[C_ROW:P:8, :], in_=c_scales[0].bitcast(I32))
        kw_all = pool.tile([P, T], I32, name="kw_all")
        nc.sync.dma_start(out=kw_all[:], in_=k_words[0].rearrange("p t r -> p (t r)").bitcast(I32))
        cw_all = pool.tile([P, T], I32, name="cw_all")
        c_cols = c_words[0].rearrange("p t r -> p (t r)").bitcast(I32)
        nc.sync.dma_start(out=cw_all[:, 0:C_CUT], in_=c_cols[:, 0:C_CUT])

        q_grouped = pool.tile([P, NQ, PACK], BF16, name="q_grouped", align_bytes=64)
        nc.scalar.copy(out=q_grouped[:].rearrange("p (c i) j -> p c j i", i=4),
                       in_=q_raw[:].rearrange("p j (c i) -> p c j i", i=4))
        ks_got = pool.tile([P, N], U8, name="ks_got")
        nc.vector.tensor_copy(ks_got[:], ks_all[:].bitcast(U8).indirect(offsets[:]))
        ks = pool.tile([P, N // 4], I32, name="ks", align_bytes=64)
        nc.vector.tensor_copy(ks[:], ks_got[:].bitcast(I32))
        for r in range(1, 4):
            nc.sync.dma_start(out=ks[r:P:32, :], in_=ks_got[8 * r:P:32, :].bitcast(I32))
        nc.sync.dma_start(out=cw_all[:, C_CUT:T], in_=c_cols[:, C_CUT:T])
        cs_got = pool.tile([P, N], U8, name="cs_got")
        nc.vector.tensor_copy(cs_got[:], cs_all[:].bitcast(U8).indirect(offsets[:]))

        q_codes = pool.tile([P, NQ], U32, name="q_codes", align_bytes=64)
        q_scales = pool.tile([P, NQ], U8, name="q_scales", align_bytes=64)
        nc.vector.quantize_mx(out=q_codes[:].bitcast(FP8X4), scales=q_scales[:],
                              in_=q_grouped[:].rearrange("p w j -> p (w j)"))
        cs = staged.tile([P, N // 4], I32, name="cs", offset=4 * N, align_bytes=64)
        nc.vector.tensor_copy(cs[:], cs_got[:].bitcast(I32))
        for r, queue in ((1, nc.sync), (2, nc.scalar), (3, nc.sync)):
            queue.dma_start(out=cs[C_ROW + r:P:32, :], in_=cs_got[C_ROW + 8 * r:P:32, :].bitcast(I32))

        kw = staged.tile([P, N], U32, name="kw", offset=0, align_bytes=64)
        for h in range(2):
            nc.vector.tensor_copy(kw[:, h * HALF:(h + 1) * HALF], kw_all[:].bitcast(U32).indirect(offsets[:, h * 16:(h + 1) * 16]))

        ks_bytes = ks[:].bitcast(U8)
        cs_bytes = cs[C_ROW:P, :].bitcast(U8)

        def scores(name, tag, b, words, scales, slots):
            acc = psum.tile([P, slots.stop - slots.start], F32, name=name, tag=tag)
            nc.tensor.matmul_mx(out=acc[:], lhsT=q_codes[:, b * P:(b + 1) * P].bitcast(FP8X4),
                                lhsT_scale=q_scales[:, b * P:(b + 1) * P],
                                rhs=words[:, slots].bitcast(FP8X4), rhs_scale=scales[:, slots], start=True, stop=True)
            return acc

        a_neg = [pool.tile([P, N], F32, name=f"a_neg{b}") for b in range(2)]
        for h in range(2):
            for b in range(2):
                a = scores(f"a{b}{h}", f"a{b}{h}", b, kw, ks_bytes, HALVES[h])
                nc.scalar.activation(out=a_neg[b][:, HALVES[h]], in_=a[:], func=ACT.Copy, scale=-1.5)

        cw = pool.tile([P, N], U32, name="cw", align_bytes=64)
        for slots in PIECES:
            nc.vector.tensor_copy(cw[:, slots], cw_all[:].bitcast(U32).indirect(offsets[:, slots.start // 16:slots.stop // 16]))

        g_neg = [pool.tile([P, N], F32, name=f"g_neg{b}") for b in range(2)]

        def combine(b, slots, tag):
            z = scores(f"z{b}_{slots.start}", tag, b, cw, cs_bytes, slots)
            nc.vector.scalar_tensor_tensor(out=g_neg[b][:, slots], in0=z[:], scalar=0.5,
                                           in1=a_neg[b][:, slots], op0=ALU.mult, op1=ALU.add)

        combine(0, PIECES[0], "z00")
        z = scores("z1_0", "z10", 1, cw, cs_bytes, HALVES[0])
        z_half = pool.tile([P, HALF], F32, name="z_half")
        nc.scalar.activation(out=z_half[:], in_=z[:], func=ACT.Copy, scale=0.5)
        nc.gpsimd.tensor_tensor(out=g_neg[1][:, HALVES[0]], in0=z_half[:], in1=a_neg[1][:, HALVES[0]], op=ALU.add)
        combine(0, PIECES[1], "z01")
        combine(0, PIECES[2], "z02")
        combine(1, HALVES[1], "a00")

        m_neg = [pool.tile([P, 1], F32, name=f"m_neg{b}") for b in range(2)]
        for b in range(2):
            nc.vector.tensor_reduce(out=m_neg[b][:], in_=g_neg[b][:], axis=AX.X, op=ALU.min)
        for b in range(2):
            e = pool.tile([P, N], F32, name=f"e{b}")
            total = pool.tile([P, 1], F32, name=f"total{b}")
            inv = pool.tile([P, 1], F32, name=f"inv{b}")
            y = pool.tile([P, N], F32, name=f"y{b}")
            nc.scalar.activation(out=e[:], in_=g_neg[b][:], func=ACT.Exp, bias=m_neg[b][:], scale=-1.0,
                                 accum_out=total[:])
            nc.vector.reciprocal(out=inv[:], in_=total[:])
            for slots in ((slice(0, N),), (slice(0, HALF), slice(HALF, N)))[b]:
                nc.vector.tensor_scalar(out=y[:, slots], in0=e[:, slots], scalar1=inv[:], scalar2=None, op0=ALU.mult)
                nc.sync.dma_start(out=out[0, b * P:(b + 1) * P, slots], in_=y[:, slots])
